import numpy as np
import ml_dtypes


def mxq(x, axis, fmt="e4m3"):
    dtype, down = {"e4m3": (ml_dtypes.float8_e4m3fn, 7), "e5m2": (ml_dtypes.float8_e5m2, 14)}[fmt]
    v = np.moveaxis(np.asarray(x, np.float32).astype(ml_dtypes.bfloat16).astype(np.float64), axis, -1)
    blocks = v.reshape(v.shape[:-1] + (-1, 32))
    amax = np.abs(blocks).max(-1, keepdims=True)
    byte = np.maximum(np.where(amax > 0, np.frexp(amax)[1] - 1 + 127, 0) - down, 1)
    scale = np.exp2(byte - 127.0)
    codes = (blocks / scale).astype(np.float32).astype(dtype).astype(np.float64)
    return np.moveaxis((codes * scale).reshape(v.shape), -1, axis)


WIDE = False


def mx_kscale(k):
    if not WIDE:
        return np.ones(k)
    levels = np.array([10, -10, 5, -5, 0])
    if k % 512:
        return np.exp2(np.random.permutation(np.resize(levels, k // 32))).repeat(32)
    a = np.empty((k // 512, 16))
    for p in range(k // 512):
        a[p, :8] = np.random.permutation(np.resize(levels, 8))
        for g in range(8):
            far = levels[np.abs(levels - a[p, g]) >= 10]
            a[p, g + 8] = far[np.random.randint(len(far))]
    return np.exp2(a.ravel()).repeat(32)


BF16 = ml_dtypes.bfloat16


def bf(x):
    return np.asarray(x, np.float32).astype(BF16)


def f64(x):
    return np.asarray(x).astype(np.float64)


E2M1 = np.array([0.0, 0.5, 1.0, 1.5, 2.0, 3.0, 4.0, 6.0, -0.0, -0.5, -1.0, -1.5, -2.0, -3.0, -4.0, -6.0])


def pack_weight(w, fmt):
    k, n = w.shape
    w = f64(bf(w)).reshape(k // 32, 32, n)
    amax = np.abs(w).max(1)
    if fmt == "e4m3":
        byte = np.frexp(amax)[1] - 1 + 127 - 7
    else:
        mant, ex = np.frexp(amax / 6.0)
        byte = np.where(mant > 0.5, ex, ex - 1) + 127
    byte = np.clip(np.where(amax > 0, byte, 1), 1, 254)
    scaled = (w * np.exp2(127.0 - byte)[:, None, :]).reshape(k, n).astype(np.float32)
    by_word = np.ascontiguousarray(scaled.reshape(k // 512, 128, 4, n).transpose(0, 1, 3, 2))
    if fmt == "e4m3":
        words = by_word.astype(ml_dtypes.float8_e4m3fn).view(np.uint8)
    else:
        c = by_word.astype(ml_dtypes.float4_e2m1fn).view(np.uint8) & 0xF
        words = c[..., 0::2] | (c[..., 1::2] << 4)
    return np.ascontiguousarray(words), np.ascontiguousarray(byte.astype(np.uint8).reshape(k // 512, 16, n))


def unpack_weight(words, scales, fmt):
    g, p, n, _ = words.shape
    if fmt == "e4m3":
        vals = np.ascontiguousarray(words).view(ml_dtypes.float8_e4m3fn).astype(np.float64)
    else:
        nib = np.empty((g, p, n, 4), np.uint8)
        nib[..., 0::2] = words & 0xF
        nib[..., 1::2] = words >> 4
        vals = E2M1[nib]
    vals = vals * np.repeat(np.exp2(scales.astype(np.float64) - 127.0), 8, axis=1)[..., None]
    return vals.transpose(0, 1, 3, 2).reshape(g * 512, n)
def pack4(w):
    words, scales = pack_weight(w, "e2m1")
    return words.reshape(words.shape[0], 128, -1), scales


def unpack4(words, scales):
    return unpack_weight(words.reshape(words.shape[0], 128, -1, 2), scales, "e2m1")


def planes(Y):
    n, m = Y.shape
    b = f64(bf(Y)).reshape(n // 32, 32, m)
    amax = np.abs(b).max(1)
    byte = np.clip(np.where(amax > 0, np.frexp(amax)[1] - 1 + 127 - 7, 1), 1, 254)
    codes = (b * np.exp2(127.0 - byte)[:, None, :]).reshape(n, m).astype(np.float32).astype(ml_dtypes.float8_e4m3fn).view(np.uint8)
    words = codes.reshape(n // 512, 128, 4, m).transpose(0, 1, 3, 2)
    return np.ascontiguousarray(words), np.ascontiguousarray(byte.astype(np.uint8).reshape(n // 512, 16, m))


U, D, A, J = 1024, 1024, 1024, 1536

def setup_inputs():
    s = mx_kscale(D)
    t = mx_kscale(A)
    r = mx_kscale(A)
    rn = np.random.randn
    F = rn(D, U)
    E = (0.5 * rn(D, A) + 0.5 * rn(D, 1)) / np.sqrt(D)
    user_words, user_scales = pack4(F * s[:, None])
    ap_words, ap_scales = pack4(E / s[:, None])
    own = np.exp(0.8 * rn(1, J)) * np.exp(1.2 * rn(A, J)) * 0.5 / A
    other = np.exp(0.4 * rn(1, J)) * np.exp(1.2 * rn(A, J)) * 0.5 / A
    return {"user_words": user_words, "user_scales": user_scales,
            "ap_words": ap_words, "ap_scales": ap_scales,
            "array_gain": bf(np.exp(0.4 * rn(A)) * t),
            "leak_gain": bf(np.exp(0.4 * rn(A)) * r),
            "own_power": bf(own / t[:, None]),
            "other_power": bf(other / r[:, None]),
            "noise_power": bf(0.5 * np.exp(0.6 * rn(U)))}

def reference(user_words, user_scales, ap_words, ap_scales, array_gain, leak_gain, own_power, other_power, noise_power):
    F = unpack4(user_words, user_scales)
    E = unpack4(ap_words, ap_scales)
    L = F.T @ E
    sq = np.exp(2.0 * L) * f64(array_gain)
    raw = np.exp(L) * f64(leak_gain)
    S = mxq(sq, 1, "e4m3") @ mxq(f64(own_power), 0, "e4m3")
    I = mxq(raw, 1, "e4m3") @ mxq(f64(other_power), 0, "e4m3")
    y = np.log(1.0 + S / (I + f64(noise_power)[:, None]))
    Y = y.reshape(U, J)
    words, scales = planes(Y)
    return y, words, scales

@@ -1,0 +1,280 @@
+from contextlib import ExitStack
+
+import concourse.mybir as mybir
+
+U, D, A, J = 1024, 1024, 1024, 1536
+FLOPS = 2 * U * D * A + 2 * 2 * U * A * J
+
+F32 = mybir.dt.float32
+BF16 = mybir.dt.bfloat16
+I32 = mybir.dt.int32
+U32 = mybir.dt.uint32
+U8 = mybir.dt.uint8
+FP8X4 = mybir.dt.float8_e4m3fn_x4
+FP4X4 = mybir.dt.float4_e2m1fn_x4
+ACT = mybir.ActivationFunctionType
+ALU = mybir.AluOpType
+
+P = 128
+PACK = 4
+GROUP = P * PACK
+N = 512
+RAW, SQ = 0, 1
+UNITS = [(0, 0), (0, 1), (1, 0), (1, 1), (0, 2), (1, 2)]
+
+
+def tile_cell_free_log_rate_k5_kernel(
+    tc, user_words, user_scales, ap_words, ap_scales, array_gain, leak_gain,
+    own_power, other_power, noise_power, out_0, out_1, out_2,
+):
+    nc = tc.nc
+    with ExitStack() as ctx:
+        keep = ctx.enter_context(tc.tile_pool(name="keep", bufs=1))
+        flow = ctx.enter_context(tc.tile_pool(name="flow", bufs=1))
+        psum = ctx.enter_context(tc.psum_pool(name="psum", bufs=1))
+        ctx.enter_context(tc.manual_schedule())
+
+        def kept(name, shape, dtype):
+            return keep.tile(shape, dtype, name=name, align_bytes=64)
+
+        def bank(number):
+            return psum.tile([P, N], F32, name="bank%d" % number, tag="bank%d" % number)
+
+        ap_plane = kept("ap_plane", [P, 2, A], U8)
+        user_plane = kept("user_plane", [P, 2, U], U8)
+        nc.vector.memset(ap_plane[:].bitcast(I32), 0)
+        nc.vector.memset(user_plane[:].bitcast(I32), 0)
+
+        def load_words(name, words, half):
+            tile = kept(name, [P, 2, 2 * GROUP], U8)
+            src = words.bitcast(I32).rearrange("g p w -> p g w")
+            nc.sync.dma_start(out=tile[:].bitcast(I32), in_=src[:, :, half * 256 : (half + 1) * 256])
+            return tile
+
+        def load_plane(plane, scales):
+            src = scales.bitcast(I32).rearrange("g r w -> r g w")
+            dst = plane[:].bitcast(I32)
+            for q in range(4):
+                nc.sync.dma_start(out=dst[32 * q : 32 * q + 4, :, :], in_=src[4 * q : 4 * q + 4, :, :])
+
+        power = {RAW: other_power, SQ: own_power}
+        power_raw = {}
+
+        def load_power(c):
+            for f in (RAW, SQ):
+                for g in range(2):
+                    tile = kept("power%d%d%d" % (f, g, c), [P, PACK, N], BF16)
+                    rows = power[f][g * GROUP : (g + 1) * GROUP, c * N : (c + 1) * N]
+                    nc.sync.dma_start(out=tile[:], in_=rows.rearrange("(p t) j -> p t j", t=PACK))
+                    power_raw[f, g, c] = tile
+
+        ap_raw = [None, None]
+        user_codes = [None, None]
+        ap_raw[0] = load_words("ap_raw0", ap_words, 0)
+        gains = kept("gains", [P, 2, 16], BF16)
+        for f, gain in ((RAW, leak_gain), (SQ, array_gain)):
+            nc.sync.dma_start(
+                out=gains[:, f, 0:8].rearrange("p (g t) -> p g t", t=PACK),
+                in_=gain.rearrange("(g p t) -> p g t", g=2, t=PACK),
+            )
+        load_plane(ap_plane, ap_scales)
+        user_codes[0] = load_words("user_codes0", user_words, 0)
+        load_plane(user_plane, user_scales)
+        ap_raw[1] = load_words("ap_raw1", ap_words, 1)
+        load_power(0)
+        user_codes[1] = load_words("user_codes1", user_words, 1)
+        noise = kept("noise", [P, 2, PACK], BF16)
+        nc.sync.dma_start(out=noise[:], in_=noise_power.rearrange("(h p s) -> p h s", h=2, s=PACK))
+        load_power(1)
+        load_power(2)
+
+        log_gain = kept("log_gain", [P, 2, 8], F32)
+        nc.scalar.activation(out=log_gain[:], in_=gains[:, :, 0:8], func=ACT.Ln)
+
+        ap_codes, ap_scale = [], []
+        for g in range(2):
+            codes = kept("ap_codes%d" % g, [P, 2, PACK, 2 * P], U8)
+            nc.vector.tensor_copy(
+                out=codes[:].rearrange("p d t (m b) -> p d t m b", b=2),
+                in_=ap_raw[g][:].rearrange("p d (m t b) -> p d t m b", t=PACK, b=2),
+            )
+            scale = kept("ap_scale%d" % g, [P, 2, PACK, P], U8)
+            nc.vector.tensor_copy(
+                out=scale[:],
+                in_=ap_plane[:, :, g * GROUP : (g + 1) * GROUP].rearrange("p d (m t) -> p d t m", t=PACK),
+            )
+            ap_codes.append(codes)
+            ap_scale.append(scale)
+
+        waiting = []
+
+        def push(*stages):
+            older = list(waiting)
+            waiting.clear()
+            if stages:
+                stages[0]()
+            for rest in older:
+                rest[0]()
+                if len(rest) > 1:
+                    waiting.append(rest[1:])
+            if len(stages) > 1:
+                waiting.append(stages[1:])
+
+        def interleave(copy, src, tag, bufs):
+            width = src.shape[2]
+            packed = flow.tile([P, width, PACK], BF16, name=tag, tag=tag, bufs=bufs, align_bytes=64)
+            copy(
+                out=packed[:].rearrange("p (c i) t -> p c t i", i=4),
+                in_=src.rearrange("p t (c i) -> p c t i", i=4),
+            )
+            return packed
+
+        def quantize(packed, codes, scales):
+            nc.vector.quantize_mx(
+                out=codes.bitcast(FP8X4), scales=scales, in_=packed[:].rearrange("p c t -> p (c t)")
+            )
+
+        def prepare(src, codes, scales):
+            box = []
+            push(
+                lambda: box.append(interleave(nc.vector.tensor_copy, src, "packed", 4)),
+                lambda: quantize(box[0], codes, scales),
+            )
+
+        power_q = {}
+
+        def prepare_power(c):
+            for f in (RAW, SQ):
+                for g in range(2):
+                    codes = kept("power_codes%d%d%d" % (f, g, c), [P, N], U32)
+                    scales = kept("power_scales%d%d%d" % (f, g, c), [P, N], U8)
+                    power_q[f, g, c] = (codes, scales)
+                    prepare(power_raw[f, g, c][:], codes[:], scales[:])
+
+        gain_bf = {}
+        gain_q = {}
+
+        def stage1(h):
+            for g in range(2):
+                for f in (RAW, SQ):
+                    gain_bf[f, g, h] = kept("gain_bf%d%d%d" % (f, g, h), [P, PACK, N], BF16)
+                for t in range(PACK):
+                    n = 8 * h + 4 * g + t
+                    logs = bank(7 - (15 - n) % 3)
+                    for d in range(2):
+                        nc.tensor.matmul_mx(
+                            out=logs[:],
+                            lhsT=ap_codes[g][:, d, t, :].bitcast(FP4X4),
+                            lhsT_scale=ap_scale[g][:, d, t, :],
+                            rhs=user_codes[h][:, d, :].bitcast(FP4X4),
+                            rhs_scale=user_plane[:, d, h * N : (h + 1) * N],
+                            start=(d == 0),
+                            stop=(d == 1),
+                        )
+                    for f, factor in ((RAW, 1.0), (SQ, 2.0)):
+                        nc.scalar.activation(
+                            out=gain_bf[f, g, h][:, t, :].rearrange("p (s m) -> p s m", s=PACK),
+                            in_=logs[:].rearrange("p (m s) -> p s m", s=PACK),
+                            func=ACT.Exp,
+                            bias=log_gain[:, f, 4 * g + t : 4 * g + t + 1],
+                            scale=factor,
+                        )
+
+        def prepare_gains(h, parts):
+            width = N // parts
+            for g in range(2):
+                for f in (RAW, SQ):
+                    codes = kept("gain_codes%d%d%d" % (f, g, h), [P, N], U32)
+                    scales = kept("gain_scales%d%d%d" % (f, g, h), [P, N], U8)
+                    gain_q[f, g, h] = (codes, scales)
+            for part in range(parts):
+                cols = slice(part * width, (part + 1) * width)
+                for g in range(2):
+                    for f in (RAW, SQ):
+                        codes, scales = gain_q[f, g, h]
+                        prepare(gain_bf[f, g, h][:, :, cols], codes[:, cols], scales[:, cols])
+
+        results = {}
+
+        def stage2(unit):
+            h, c = UNITS[unit]
+            log_den = flow.tile([P, PACK, N], F32, name="log_den", tag="log_den", bufs=3)
+            y = flow.tile([P, PACK, N], F32, name="y", tag="y", bufs=4)
+            results[unit] = (log_den, y)
+            for s in range(PACK):
+                users = slice(s * P, (s + 1) * P)
+                den, num = bank(2 * s), bank(2 * s + 1)
+                for acc, terms, dst in ((den, (RAW,), log_den), (num, (RAW, SQ), y)):
+                    passes = [(f, g) for f in terms for g in range(2)]
+                    for k, (f, g) in enumerate(passes):
+                        nc.tensor.matmul_mx(
+                            out=acc[:],
+                            lhsT=gain_q[f, g, h][0][:, users].bitcast(FP8X4),
+                            lhsT_scale=gain_q[f, g, h][1][:, users],
+                            rhs=power_q[f, g, c][0][:].bitcast(FP8X4),
+                            rhs_scale=power_q[f, g, c][1][:],
+                            start=(k == 0),
+                            stop=(k == len(passes) - 1),
+                        )
+                    nc.scalar.activation(
+                        out=dst[:, s, :], in_=acc[:], func=ACT.Ln, bias=noise[:, h, s : s + 1]
+                    )
+
+        y_scales = [kept("y_scales%d" % h, [P, J], U8) for h in range(2)]
+
+        def finish(unit, parts):
+            h, c = UNITS[unit]
+            log_den, y = results[unit]
+            cols = slice(c * N, (c + 1) * N)
+            rows = out_0[h * GROUP : (h + 1) * GROUP, cols].rearrange("(p s) j -> p s j", s=PACK)
+            step = PACK // parts
+
+            def subtract(part):
+                slots = slice(part * step, (part + 1) * step)
+                nc.vector.tensor_tensor(
+                    out=y[:, slots, :], in0=y[:, slots, :], in1=log_den[:, slots, :], op=ALU.subtract
+                )
+                nc.sync.dma_start(out=rows[:, slots, :], in_=y[:, slots, :])
+
+            box = []
+
+            def planes():
+                codes = flow.tile([P, N], U32, name="y_codes", tag="y_codes", bufs=3, align_bytes=64)
+                quantize(box[0], codes[:], y_scales[h][:, cols])
+                words = out_1[h].rearrange("p m t -> p (m t)").bitcast(I32)
+                nc.sync.dma_start(out=words[:, cols], in_=codes[:].bitcast(I32))
+                if c == 2:
+                    src = y_scales[h][:].bitcast(I32)
+                    dst = out_2[h].bitcast(I32)
+                    for q in range(4):
+                        nc.sync.dma_start(out=dst[4 * q : 4 * q + 4, :], in_=src[32 * q : 32 * q + 4, :])
+
+            for part in range(parts - 1):
+                push(lambda part=part: subtract(part))
+            push(
+                lambda: subtract(parts - 1),
+                lambda: box.append(interleave(nc.vector.tensor_copy, y[:], "packed", 4)),
+                planes,
+            )
+
+        prepare_power(0)
+        stage1(0)
+        prepare_gains(0, 1)
+        prepare_power(1)
+        stage1(1)
+        prepare_gains(1, 2)
+        stage2(0)
+        stage2(1)
+        finish(0, 2)
+        finish(1, 2)
+        stage2(2)
+        prepare_power(2)
+        stage2(3)
+        finish(2, 2)
+        stage2(4)
+        finish(3, 2)
+        finish(4, 2)
+        stage2(5)
+        finish(5, 4)
+        push()
+        push()

@@ -20,7 +20,13 @@ PACK = 4
 GROUP = P * PACK
 N = 512
 RAW, SQ = 0, 1
-UNITS = [(0, 0), (0, 1), (1, 0), (1, 1), (0, 2), (1, 2)]
+W = 256
+UNITS = [(0, 0), (0, 1), (1, 0), (1, 1)] + [(h, k) for k in range(2, 6) for h in range(2)]
+HELP_FIRST = 4
+HELP_EVERY = 5
+SHARE = {3: 2, 4: 2, 5: 2}
+LOG_BUFS = 6
+GAIN_BUFS = 8
 
 
 def tile_cell_free_log_rate_k5_kernel(
@@ -42,7 +48,7 @@ def tile_cell_free_log_rate_k5_kernel(
 
         ap_plane = kept("ap_plane", [P, 2, A], U8)
         user_plane = kept("user_plane", [P, 2, U], U8)
-        nc.vector.memset(ap_plane[:].bitcast(I32), 0)
+        nc.gpsimd.memset(ap_plane[:].bitcast(I32), 0)
         nc.vector.memset(user_plane[:].bitcast(I32), 0)
 
         def load_words(name, words, half):
@@ -68,9 +74,7 @@ def tile_cell_free_log_rate_k5_kernel(
                     nc.sync.dma_start(out=tile[:], in_=rows.rearrange("(p t) j -> p t j", t=PACK))
                     power_raw[f, g, c] = tile
 
-        ap_raw = [None, None]
         user_codes = [None, None]
-        ap_raw[0] = load_words("ap_raw0", ap_words, 0)
         gains = kept("gains", [P, 2, 16], BF16)
         for f, gain in ((RAW, leak_gain), (SQ, array_gain)):
             nc.sync.dma_start(
@@ -78,9 +82,10 @@ def tile_cell_free_log_rate_k5_kernel(
                 in_=gain.rearrange("(g p t) -> p g t", g=2, t=PACK),
             )
         load_plane(ap_plane, ap_scales)
+        ap_raw = [load_words("ap_raw0", ap_words, 0)]
         user_codes[0] = load_words("user_codes0", user_words, 0)
         load_plane(user_plane, user_scales)
-        ap_raw[1] = load_words("ap_raw1", ap_words, 1)
+        ap_raw.append(load_words("ap_raw1", ap_words, 1))
         load_power(0)
         user_codes[1] = load_words("user_codes1", user_words, 1)
         noise = kept("noise", [P, 2, PACK], BF16)
@@ -91,20 +96,17 @@ def tile_cell_free_log_rate_k5_kernel(
         log_gain = kept("log_gain", [P, 2, 8], F32)
         nc.scalar.activation(out=log_gain[:], in_=gains[:, :, 0:8], func=ACT.Ln)
 
-        ap_codes, ap_scale = [], []
-        for g in range(2):
-            codes = kept("ap_codes%d" % g, [P, 2, PACK, 2 * P], U8)
+        ap_codes = [kept("ap_codes%d" % g, [P, 2, PACK, 2 * P], U8) for g in range(2)]
+        ap_scale = [kept("ap_scale%d" % g, [P, 2, PACK, P], U8) for g in range(2)]
+        for g, slots in ((0, slice(0, 1)), (0, slice(1, PACK)), (1, slice(0, PACK))):
             nc.vector.tensor_copy(
-                out=codes[:].rearrange("p d t (m b) -> p d t m b", b=2),
-                in_=ap_raw[g][:].rearrange("p d (m t b) -> p d t m b", t=PACK, b=2),
+                out=ap_scale[g][:, :, slots, :],
+                in_=ap_plane[:, :, g * GROUP : (g + 1) * GROUP].rearrange("p d (m t) -> p d t m", t=PACK)[:, :, slots, :],
             )
-            scale = kept("ap_scale%d" % g, [P, 2, PACK, P], U8)
             nc.vector.tensor_copy(
-                out=scale[:],
-                in_=ap_plane[:, :, g * GROUP : (g + 1) * GROUP].rearrange("p d (m t) -> p d t m", t=PACK),
+                out=ap_codes[g][:].rearrange("p d t (m b) -> p d t m b", b=2)[:, :, slots],
+                in_=ap_raw[g][:].rearrange("p d (m t b) -> p d t m b", t=PACK, b=2)[:, :, slots],
             )
-            ap_codes.append(codes)
-            ap_scale.append(scale)
 
         waiting = []
 
@@ -120,14 +122,18 @@ def tile_cell_free_log_rate_k5_kernel(
             if len(stages) > 1:
                 waiting.append(stages[1:])
 
-        def interleave(copy, src, tag, bufs):
-            width = src.shape[2]
-            packed = flow.tile([P, width, PACK], BF16, name=tag, tag=tag, bufs=bufs, align_bytes=64)
+        def interleave(copy, src, dst):
             copy(
-                out=packed[:].rearrange("p (c i) t -> p c t i", i=4),
+                out=dst.rearrange("p (c i) t -> p c t i", i=4),
                 in_=src.rearrange("p t (c i) -> p c t i", i=4),
             )
+
+        def vector_interleave(src):
+            packed = flow.tile([P, src.shape[2], PACK], BF16, name="packed", tag="packed", bufs=4, align_bytes=64)
+            interleave(nc.vector.tensor_copy, src, packed[:])
             return packed
+
+        scalar_jobs = []
 
         def quantize(packed, codes, scales):
             nc.vector.quantize_mx(
@@ -137,19 +143,44 @@ def tile_cell_free_log_rate_k5_kernel(
         def prepare(src, codes, scales):
             box = []
             push(
-                lambda: box.append(interleave(nc.vector.tensor_copy, src, "packed", 4)),
+                lambda: box.append(vector_interleave(src)),
                 lambda: quantize(box[0], codes, scales),
             )
 
         power_q = {}
 
-        def prepare_power(c):
-            for f in (RAW, SQ):
-                for g in range(2):
-                    codes = kept("power_codes%d%d%d" % (f, g, c), [P, N], U32)
-                    scales = kept("power_scales%d%d%d" % (f, g, c), [P, N], U8)
-                    power_q[f, g, c] = (codes, scales)
-                    prepare(power_raw[f, g, c][:], codes[:], scales[:])
+        order = [(f, g) for f in (RAW, SQ) for g in range(2)]
+        for c in range(3):
+            for f, g in order:
+                codes = kept("power_codes%d%d%d" % (f, g, c), [P, N], U32)
+                scales = kept("power_scales%d%d%d" % (f, g, c), [P, N], U8)
+                power_q[f, g, c] = (codes, scales)
+
+        def piece(k):
+            return k // 2, slice(k % 2 * W, (k % 2 + 1) * W)
+
+        def prepare_power(c, cols, which):
+            for f, g in which:
+                codes, scales = power_q[f, g, c]
+                prepare(power_raw[f, g, c][:, :, cols], codes[:, cols], scales[:, cols])
+
+        helped = {}
+
+        def enlist_scalar(k):
+            c, cols = piece(k)
+            for f, g in order[: SHARE[k]]:
+                packed = flow.tile([P, W, PACK], BF16, name="helped", tag="helped", bufs=6, align_bytes=64)
+                helped[k, f, g] = packed
+                scalar_jobs.append(
+                    lambda src=power_raw[f, g, c][:, :, cols], dst=packed[:]: interleave(nc.scalar.copy, src, dst)
+                )
+
+        def prepare_helped(k):
+            c, cols = piece(k)
+            prepare_power(c, cols, order[SHARE[k] :])
+            for f, g in order[: SHARE[k]]:
+                codes, scales = power_q[f, g, c]
+                push(lambda: quantize(helped[k, f, g], codes[:, cols], scales[:, cols]))
 
         gain_bf = {}
         gain_q = {}
@@ -157,10 +188,12 @@ def tile_cell_free_log_rate_k5_kernel(
         def stage1(h):
             for g in range(2):
                 for f in (RAW, SQ):
-                    gain_bf[f, g, h] = kept("gain_bf%d%d%d" % (f, g, h), [P, PACK, N], BF16)
+                    gain_bf[f, g, h] = flow.tile(
+                        [P, PACK, N], BF16, name="gain_bf", tag="gain_bf", bufs=GAIN_BUFS, align_bytes=64
+                    )
                 for t in range(PACK):
                     n = 8 * h + 4 * g + t
-                    logs = bank(7 - (15 - n) % 3)
+                    logs = bank(4 + n % 4)
                     for d in range(2):
                         nc.tensor.matmul_mx(
                             out=logs[:],
@@ -180,16 +213,14 @@ def tile_cell_free_log_rate_k5_kernel(
                             scale=factor,
                         )
 
-        def prepare_gains(h, parts):
-            width = N // parts
-            for g in range(2):
+        def prepare_gains(h):
+            for g, parts in ((0, 1), (1, 2)):
                 for f in (RAW, SQ):
                     codes = kept("gain_codes%d%d%d" % (f, g, h), [P, N], U32)
                     scales = kept("gain_scales%d%d%d" % (f, g, h), [P, N], U8)
                     gain_q[f, g, h] = (codes, scales)
-            for part in range(parts):
-                cols = slice(part * width, (part + 1) * width)
-                for g in range(2):
+                for part in range(parts):
+                    cols = slice(part * N // parts, (part + 1) * N // parts)
                     for f in (RAW, SQ):
                         codes, scales = gain_q[f, g, h]
                         prepare(gain_bf[f, g, h][:, :, cols], codes[:, cols], scales[:, cols])
@@ -197,84 +228,115 @@ def tile_cell_free_log_rate_k5_kernel(
         results = {}
 
         def stage2(unit):
-            h, c = UNITS[unit]
-            log_den = flow.tile([P, PACK, N], F32, name="log_den", tag="log_den", bufs=3)
-            y = flow.tile([P, PACK, N], F32, name="y", tag="y", bufs=4)
-            results[unit] = (log_den, y)
+            h, k = UNITS[unit]
+            c, cols = piece(k)
+            logs = flow.tile([P, PACK, 2, W], F32, name="logs", tag="logs", bufs=LOG_BUFS)
+            results[unit] = logs
             for s in range(PACK):
                 users = slice(s * P, (s + 1) * P)
-                den, num = bank(2 * s), bank(2 * s + 1)
-                for acc, terms, dst in ((den, (RAW,), log_den), (num, (RAW, SQ), y)):
+                slot = PACK * unit + s
+                acc = bank(slot % 8)
+                for side, terms in enumerate(((RAW,), (RAW, SQ))):
                     passes = [(f, g) for f in terms for g in range(2)]
-                    for k, (f, g) in enumerate(passes):
+                    for n, (f, g) in enumerate(passes):
                         nc.tensor.matmul_mx(
-                            out=acc[:],
+                            out=acc[:, side * W : (side + 1) * W],
                             lhsT=gain_q[f, g, h][0][:, users].bitcast(FP8X4),
                             lhsT_scale=gain_q[f, g, h][1][:, users],
-                            rhs=power_q[f, g, c][0][:].bitcast(FP8X4),
-                            rhs_scale=power_q[f, g, c][1][:],
-                            start=(k == 0),
-                            stop=(k == len(passes) - 1),
+                            rhs=power_q[f, g, c][0][:, cols].bitcast(FP8X4),
+                            rhs_scale=power_q[f, g, c][1][:, cols],
+                            start=(n == 0),
+                            stop=(n == len(passes) - 1),
                         )
-                    nc.scalar.activation(
-                        out=dst[:, s, :], in_=acc[:], func=ACT.Ln, bias=noise[:, h, s : s + 1]
-                    )
-
-        y_scales = [kept("y_scales%d" % h, [P, J], U8) for h in range(2)]
-
-        def finish(unit, parts):
-            h, c = UNITS[unit]
-            log_den, y = results[unit]
-            cols = slice(c * N, (c + 1) * N)
-            rows = out_0[h * GROUP : (h + 1) * GROUP, cols].rearrange("(p s) j -> p s j", s=PACK)
-            step = PACK // parts
-
-            def subtract(part):
-                slots = slice(part * step, (part + 1) * step)
-                nc.vector.tensor_tensor(
-                    out=y[:, slots, :], in0=y[:, slots, :], in1=log_den[:, slots, :], op=ALU.subtract
+                nc.scalar.activation(
+                    out=logs[:, s].rearrange("p e j -> p (e j)"), in_=acc[:], func=ACT.Ln, bias=noise[:, h, s : s + 1]
                 )
+                if scalar_jobs and slot >= HELP_FIRST and (slot - HELP_FIRST) % HELP_EVERY == 0:
+                    scalar_jobs.pop(0)()
+
+        y_scales = kept("y_scales", [P, 2, J], U8)
+
+        def store_scales(queue, cols):
+            src = y_scales[:, :, cols].bitcast(I32)
+            dst = out_2[:, :, cols].bitcast(I32).rearrange("h r w -> r h w")
+            for q in range(4):
+                queue.dma_start(out=dst[4 * q : 4 * q + 4], in_=src[32 * q : 32 * q + 4])
+
+        def epilogue(unit):
+            h, k = UNITS[unit]
+            log_den, y = results[unit][:, :, 0, :], results[unit][:, :, 1, :]
+            cols = slice(k * W, (k + 1) * W)
+            rows = out_0[h * GROUP : (h + 1) * GROUP, cols].rearrange("(p s) j -> p s j", s=PACK)
+            packed = []
+
+            def subtract(slots, part):
+                nc.vector.tensor_tensor(
+                    out=y[:, slots, part], in0=y[:, slots, part], in1=log_den[:, slots, part], op=ALU.subtract
+                )
+
+            def store(slots):
                 nc.sync.dma_start(out=rows[:, slots, :], in_=y[:, slots, :])
 
-            box = []
+            def pack(part, copy=nc.vector.tensor_copy):
+                if not packed:
+                    packed.append(flow.tile([P, W, PACK], BF16, name="packed", tag="packed", bufs=4, align_bytes=64))
+                interleave(copy, y[:, :, part], packed[0][:, part, :])
 
             def planes():
-                codes = flow.tile([P, N], U32, name="y_codes", tag="y_codes", bufs=3, align_bytes=64)
-                quantize(box[0], codes[:], y_scales[h][:, cols])
+                codes = flow.tile([P, W], U32, name="y_codes", tag="y_codes", bufs=3, align_bytes=64)
+                quantize(packed[0], codes[:], y_scales[:, h, cols])
                 words = out_1[h].rearrange("p m t -> p (m t)").bitcast(I32)
                 nc.sync.dma_start(out=words[:, cols], in_=codes[:].bitcast(I32))
-                if c == 2:
-                    src = y_scales[h][:].bitcast(I32)
-                    dst = out_2[h].bitcast(I32)
-                    for q in range(4):
-                        nc.sync.dma_start(out=dst[4 * q : 4 * q + 4, :], in_=src[32 * q : 32 * q + 4, :])
 
-            for part in range(parts - 1):
-                push(lambda part=part: subtract(part))
-            push(
-                lambda: subtract(parts - 1),
-                lambda: box.append(interleave(nc.vector.tensor_copy, y[:], "packed", 4)),
-                planes,
-            )
+            return subtract, store, pack, planes
 
-        prepare_power(0)
+        every = slice(None)
+
+        def finish(unit):
+            subtract, store, pack, planes = epilogue(unit)
+
+            def first():
+                subtract(every, every)
+                store(every)
+
+            push(first, lambda: pack(every), planes)
+
+        def finish_last_two(unit):
+            subtract_a, store_a, pack_a, planes_a = epilogue(unit)
+            subtract, store, pack, planes = epilogue(unit + 1)
+            last = slice(PACK - 1, PACK)
+            left, right = slice(0, W // 2), slice(W // 2, W)
+            push(lambda: subtract_a(every, every))
+            store_a(every)
+            pack_a(every, nc.scalar.copy)
+            push(lambda: subtract(slice(0, 2), every))
+            store(slice(0, 2))
+            subtract(slice(2, 3), every)
+            subtract(last, left)
+            subtract(last, right)
+            store(slice(2, 4))
+            pack(left)
+            pack(right)
+            planes_a()
+            planes()
+
+        prepare_power(0, slice(0, N), order)
         stage1(0)
-        prepare_gains(0, 1)
-        prepare_power(1)
+        prepare_gains(0)
         stage1(1)
-        prepare_gains(1, 2)
-        stage2(0)
-        stage2(1)
-        finish(0, 2)
-        finish(1, 2)
-        stage2(2)
-        prepare_power(2)
-        stage2(3)
-        finish(2, 2)
-        stage2(4)
-        finish(3, 2)
-        finish(4, 2)
-        stage2(5)
-        finish(5, 4)
-        push()
-        push()
+        prepare_gains(1)
+        prepare_power(1, slice(0, W), order)
+        for k in range(3, 6):
+            enlist_scalar(k)
+        for unit in range(4):
+            stage2(unit)
+        last = len(UNITS) - 1
+        for unit in range(last - 1):
+            finish(unit)
+            if unit + 4 <= last:
+                stage2(unit + 4)
+            if unit in (1, 3, 5):
+                prepare_helped(3 + unit // 2)
+        store_scales(nc.sync, slice(0, J - 2 * W))
+        finish_last_two(last - 1)
+        store_scales(nc.scalar, slice(J - 2 * W, J))

from contextlib import ExitStack

import concourse.mybir as mybir

U, D, A, J = 1024, 1024, 1024, 1536
FLOPS = 2 * U * D * A + 2 * 2 * U * A * J

F32 = mybir.dt.float32
BF16 = mybir.dt.bfloat16
I32 = mybir.dt.int32
U32 = mybir.dt.uint32
U8 = mybir.dt.uint8
FP8X4 = mybir.dt.float8_e4m3fn_x4
FP4X4 = mybir.dt.float4_e2m1fn_x4
ACT = mybir.ActivationFunctionType
ALU = mybir.AluOpType

P = 128
PACK = 4
GROUP = P * PACK
N = 512
RAW, SQ = 0, 1
W = 256
UNITS = [(0, 0), (0, 1), (1, 0), (1, 1)] + [(h, k) for k in range(2, 6) for h in range(2)]
HELP_FIRST = 4
HELP_EVERY = 5
SHARE = {3: 2, 4: 2, 5: 2}
LOG_BUFS = 6
GAIN_BUFS = 8


def tile_cell_free_log_rate_k5_kernel(
    tc, user_words, user_scales, ap_words, ap_scales, array_gain, leak_gain,
    own_power, other_power, noise_power, out_0, out_1, out_2,
):
    nc = tc.nc
    with ExitStack() as ctx:
        keep = ctx.enter_context(tc.tile_pool(name="keep", bufs=1))
        flow = ctx.enter_context(tc.tile_pool(name="flow", bufs=1))
        psum = ctx.enter_context(tc.psum_pool(name="psum", bufs=1))
        ctx.enter_context(tc.manual_schedule())

        def kept(name, shape, dtype):
            return keep.tile(shape, dtype, name=name, align_bytes=64)

        def bank(number):
            return psum.tile([P, N], F32, name="bank%d" % number, tag="bank%d" % number)

        ap_plane = kept("ap_plane", [P, 2, A], U8)
        user_plane = kept("user_plane", [P, 2, U], U8)
        nc.gpsimd.memset(ap_plane[:].bitcast(I32), 0)
        nc.vector.memset(user_plane[:].bitcast(I32), 0)

        def load_words(name, words, half):
            tile = kept(name, [P, 2, 2 * GROUP], U8)
            src = words.bitcast(I32).rearrange("g p w -> p g w")
            nc.sync.dma_start(out=tile[:].bitcast(I32), in_=src[:, :, half * 256 : (half + 1) * 256])
            return tile

        def load_plane(plane, scales):
            src = scales.bitcast(I32).rearrange("g r w -> r g w")
            dst = plane[:].bitcast(I32)
            for q in range(4):
                nc.sync.dma_start(out=dst[32 * q : 32 * q + 4, :, :], in_=src[4 * q : 4 * q + 4, :, :])

        power = {RAW: other_power, SQ: own_power}
        power_raw = {}

        def load_power(c):
            for f in (RAW, SQ):
                for g in range(2):
                    tile = kept("power%d%d%d" % (f, g, c), [P, PACK, N], BF16)
                    rows = power[f][g * GROUP : (g + 1) * GROUP, c * N : (c + 1) * N]
                    nc.sync.dma_start(out=tile[:], in_=rows.rearrange("(p t) j -> p t j", t=PACK))
                    power_raw[f, g, c] = tile

        user_codes = [None, None]
        gains = kept("gains", [P, 2, 16], BF16)
        for f, gain in ((RAW, leak_gain), (SQ, array_gain)):
            nc.sync.dma_start(
                out=gains[:, f, 0:8].rearrange("p (g t) -> p g t", t=PACK),
                in_=gain.rearrange("(g p t) -> p g t", g=2, t=PACK),
            )
        load_plane(ap_plane, ap_scales)
        ap_raw = [load_words("ap_raw0", ap_words, 0)]
        user_codes[0] = load_words("user_codes0", user_words, 0)
        load_plane(user_plane, user_scales)
        ap_raw.append(load_words("ap_raw1", ap_words, 1))
        load_power(0)
        user_codes[1] = load_words("user_codes1", user_words, 1)
        noise = kept("noise", [P, 2, PACK], BF16)
        nc.sync.dma_start(out=noise[:], in_=noise_power.rearrange("(h p s) -> p h s", h=2, s=PACK))
        load_power(1)
        load_power(2)

        log_gain = kept("log_gain", [P, 2, 8], F32)
        nc.scalar.activation(out=log_gain[:], in_=gains[:, :, 0:8], func=ACT.Ln)

        ap_codes = [kept("ap_codes%d" % g, [P, 2, PACK, 2 * P], U8) for g in range(2)]
        ap_scale = [kept("ap_scale%d" % g, [P, 2, PACK, P], U8) for g in range(2)]
        for g, slots in ((0, slice(0, 1)), (0, slice(1, PACK)), (1, slice(0, PACK))):
            nc.vector.tensor_copy(
                out=ap_scale[g][:, :, slots, :],
                in_=ap_plane[:, :, g * GROUP : (g + 1) * GROUP].rearrange("p d (m t) -> p d t m", t=PACK)[:, :, slots, :],
            )
            nc.vector.tensor_copy(
                out=ap_codes[g][:].rearrange("p d t (m b) -> p d t m b", b=2)[:, :, slots],
                in_=ap_raw[g][:].rearrange("p d (m t b) -> p d t m b", t=PACK, b=2)[:, :, slots],
            )

        waiting = []

        def push(*stages):
            older = list(waiting)
            waiting.clear()
            if stages:
                stages[0]()
            for rest in older:
                rest[0]()
                if len(rest) > 1:
                    waiting.append(rest[1:])
            if len(stages) > 1:
                waiting.append(stages[1:])

        def interleave(copy, src, dst):
            copy(
                out=dst.rearrange("p (c i) t -> p c t i", i=4),
                in_=src.rearrange("p t (c i) -> p c t i", i=4),
            )

        def vector_interleave(src):
            packed = flow.tile([P, src.shape[2], PACK], BF16, name="packed", tag="packed", bufs=4, align_bytes=64)
            interleave(nc.vector.tensor_copy, src, packed[:])
            return packed

        scalar_jobs = []

        def quantize(packed, codes, scales):
            nc.vector.quantize_mx(
                out=codes.bitcast(FP8X4), scales=scales, in_=packed[:].rearrange("p c t -> p (c t)")
            )

        def prepare(src, codes, scales):
            box = []
            push(
                lambda: box.append(vector_interleave(src)),
                lambda: quantize(box[0], codes, scales),
            )

        power_q = {}

        order = [(f, g) for f in (RAW, SQ) for g in range(2)]
        for c in range(3):
            for f, g in order:
                codes = kept("power_codes%d%d%d" % (f, g, c), [P, N], U32)
                scales = kept("power_scales%d%d%d" % (f, g, c), [P, N], U8)
                power_q[f, g, c] = (codes, scales)

        def piece(k):
            return k // 2, slice(k % 2 * W, (k % 2 + 1) * W)

        def prepare_power(c, cols, which):
            for f, g in which:
                codes, scales = power_q[f, g, c]
                prepare(power_raw[f, g, c][:, :, cols], codes[:, cols], scales[:, cols])

        helped = {}

        def enlist_scalar(k):
            c, cols = piece(k)
            for f, g in order[: SHARE[k]]:
                packed = flow.tile([P, W, PACK], BF16, name="helped", tag="helped", bufs=6, align_bytes=64)
                helped[k, f, g] = packed
                scalar_jobs.append(
                    lambda src=power_raw[f, g, c][:, :, cols], dst=packed[:]: interleave(nc.scalar.copy, src, dst)
                )

        def prepare_helped(k):
            c, cols = piece(k)
            prepare_power(c, cols, order[SHARE[k] :])
            for f, g in order[: SHARE[k]]:
                codes, scales = power_q[f, g, c]
                push(lambda: quantize(helped[k, f, g], codes[:, cols], scales[:, cols]))

        gain_bf = {}
        gain_q = {}

        def stage1(h):
            for g in range(2):
                for f in (RAW, SQ):
                    gain_bf[f, g, h] = flow.tile(
                        [P, PACK, N], BF16, name="gain_bf", tag="gain_bf", bufs=GAIN_BUFS, align_bytes=64
                    )
                for t in range(PACK):
                    n = 8 * h + 4 * g + t
                    logs = bank(4 + n % 4)
                    for d in range(2):
                        nc.tensor.matmul_mx(
                            out=logs[:],
                            lhsT=ap_codes[g][:, d, t, :].bitcast(FP4X4),
                            lhsT_scale=ap_scale[g][:, d, t, :],
                            rhs=user_codes[h][:, d, :].bitcast(FP4X4),
                            rhs_scale=user_plane[:, d, h * N : (h + 1) * N],
                            start=(d == 0),
                            stop=(d == 1),
                        )
                    for f, factor in ((RAW, 1.0), (SQ, 2.0)):
                        nc.scalar.activation(
                            out=gain_bf[f, g, h][:, t, :].rearrange("p (s m) -> p s m", s=PACK),
                            in_=logs[:].rearrange("p (m s) -> p s m", s=PACK),
                            func=ACT.Exp,
                            bias=log_gain[:, f, 4 * g + t : 4 * g + t + 1],
                            scale=factor,
                        )

        def prepare_gains(h):
            for g, parts in ((0, 1), (1, 2)):
                for f in (RAW, SQ):
                    codes = kept("gain_codes%d%d%d" % (f, g, h), [P, N], U32)
                    scales = kept("gain_scales%d%d%d" % (f, g, h), [P, N], U8)
                    gain_q[f, g, h] = (codes, scales)
                for part in range(parts):
                    cols = slice(part * N // parts, (part + 1) * N // parts)
                    for f in (RAW, SQ):
                        codes, scales = gain_q[f, g, h]
                        prepare(gain_bf[f, g, h][:, :, cols], codes[:, cols], scales[:, cols])

        results = {}

        def stage2(unit):
            h, k = UNITS[unit]
            c, cols = piece(k)
            logs = flow.tile([P, PACK, 2, W], F32, name="logs", tag="logs", bufs=LOG_BUFS)
            results[unit] = logs
            for s in range(PACK):
                users = slice(s * P, (s + 1) * P)
                slot = PACK * unit + s
                acc = bank(slot % 8)
                for side, terms in enumerate(((RAW,), (RAW, SQ))):
                    passes = [(f, g) for f in terms for g in range(2)]
                    for n, (f, g) in enumerate(passes):
                        nc.tensor.matmul_mx(
                            out=acc[:, side * W : (side + 1) * W],
                            lhsT=gain_q[f, g, h][0][:, users].bitcast(FP8X4),
                            lhsT_scale=gain_q[f, g, h][1][:, users],
                            rhs=power_q[f, g, c][0][:, cols].bitcast(FP8X4),
                            rhs_scale=power_q[f, g, c][1][:, cols],
                            start=(n == 0),
                            stop=(n == len(passes) - 1),
                        )
                nc.scalar.activation(
                    out=logs[:, s].rearrange("p e j -> p (e j)"), in_=acc[:], func=ACT.Ln, bias=noise[:, h, s : s + 1]
                )
                if scalar_jobs and slot >= HELP_FIRST and (slot - HELP_FIRST) % HELP_EVERY == 0:
                    scalar_jobs.pop(0)()

        y_scales = kept("y_scales", [P, 2, J], U8)

        def store_scales(queue, cols):
            src = y_scales[:, :, cols].bitcast(I32)
            dst = out_2[:, :, cols].bitcast(I32).rearrange("h r w -> r h w")
            for q in range(4):
                queue.dma_start(out=dst[4 * q : 4 * q + 4], in_=src[32 * q : 32 * q + 4])

        def epilogue(unit):
            h, k = UNITS[unit]
            log_den, y = results[unit][:, :, 0, :], results[unit][:, :, 1, :]
            cols = slice(k * W, (k + 1) * W)
            rows = out_0[h * GROUP : (h + 1) * GROUP, cols].rearrange("(p s) j -> p s j", s=PACK)
            packed = []

            def subtract(slots, part):
                nc.vector.tensor_tensor(
                    out=y[:, slots, part], in0=y[:, slots, part], in1=log_den[:, slots, part], op=ALU.subtract
                )

            def store(slots):
                nc.sync.dma_start(out=rows[:, slots, :], in_=y[:, slots, :])

            def pack(part, copy=nc.vector.tensor_copy):
                if not packed:
                    packed.append(flow.tile([P, W, PACK], BF16, name="packed", tag="packed", bufs=4, align_bytes=64))
                interleave(copy, y[:, :, part], packed[0][:, part, :])

            def planes():
                codes = flow.tile([P, W], U32, name="y_codes", tag="y_codes", bufs=3, align_bytes=64)
                quantize(packed[0], codes[:], y_scales[:, h, cols])
                words = out_1[h].rearrange("p m t -> p (m t)").bitcast(I32)
                nc.sync.dma_start(out=words[:, cols], in_=codes[:].bitcast(I32))

            return subtract, store, pack, planes

        every = slice(None)

        def finish(unit):
            subtract, store, pack, planes = epilogue(unit)

            def first():
                subtract(every, every)
                store(every)

            push(first, lambda: pack(every), planes)

        def finish_last_two(unit):
            subtract_a, store_a, pack_a, planes_a = epilogue(unit)
            subtract, store, pack, planes = epilogue(unit + 1)
            last = slice(PACK - 1, PACK)
            left, right = slice(0, W // 2), slice(W // 2, W)
            push(lambda: subtract_a(every, every))
            store_a(every)
            pack_a(every, nc.scalar.copy)
            push(lambda: subtract(slice(0, 2), every))
            store(slice(0, 2))
            subtract(slice(2, 3), every)
            subtract(last, left)
            subtract(last, right)
            store(slice(2, 4))
            pack(left)
            pack(right)
            planes_a()
            planes()

        prepare_power(0, slice(0, N), order)
        stage1(0)
        prepare_gains(0)
        stage1(1)
        prepare_gains(1)
        prepare_power(1, slice(0, W), order)
        for k in range(3, 6):
            enlist_scalar(k)
        for unit in range(4):
            stage2(unit)
        last = len(UNITS) - 1
        for unit in range(last - 1):
            finish(unit)
            if unit + 4 <= last:
                stage2(unit + 4)
            if unit in (1, 3, 5):
                prepare_helped(3 + unit // 2)
        store_scales(nc.sync, slice(0, J - 2 * W))
        finish_last_two(last - 1)
        store_scales(nc.scalar, slice(J - 2 * W, J))
